import numpy as np
import ml_dtypes


def mxq(x, axis, fmt="e4m3"):
    dtype, down = {"e4m3": (ml_dtypes.float8_e4m3fn, 7), "e5m2": (ml_dtypes.float8_e5m2, 14)}[fmt]
    v = np.moveaxis(np.asarray(x, np.float32).astype(ml_dtypes.bfloat16).astype(np.float64), axis, -1)
    blocks = v.reshape(v.shape[:-1] + (-1, 32))
    amax = np.abs(blocks).max(-1, keepdims=True)
    byte = np.maximum(np.where(amax > 0, np.frexp(amax)[1] - 1 + 127, 0) - down, 1)
    scale = np.exp2(byte - 127.0)
    codes = (blocks / scale).astype(np.float32).astype(dtype).astype(np.float64)
    return np.moveaxis((codes * scale).reshape(v.shape), -1, axis)


WIDE = False


def mx_kscale(k):
    if not WIDE:
        return np.ones(k)
    levels = np.array([30, -30])
    if k % 512:
        return np.exp2(np.random.permutation(np.resize(levels, k // 32))).repeat(32)
    a = np.empty((k // 512, 16))
    for p in range(k // 512):
        a[p, :8] = np.random.permutation(np.resize(levels, 8))
        for g in range(8):
            far = levels[np.abs(levels - a[p, g]) >= 10]
            a[p, g + 8] = far[np.random.randint(len(far))]
    return np.exp2(a.ravel()).repeat(32)


def f64(x):
    return np.asarray(x).astype(np.float64)


K, M, T = 512, 2048, 1536


def setup_inputs():
    n = np.random.standard_normal
    s1 = mx_kscale(K)[:, None]
    s2 = mx_kscale(K)[:, None]
    return {
        "w": (n((K, M)) / np.sqrt(K) * s1).astype(np.float32),
        "xd": (n((K, T)) / s1).astype(np.float32),
        "wd": (n((K, M)) / np.sqrt(K) * s2).astype(np.float32),
        "x": (n((K, T)) / s2).astype(np.float32),
    }


def reference(w, xd, wd, x):
    w_ = mxq(f64(w), 0, "e4m3")
    xd_ = mxq(f64(xd), 0, "e5m2")
    wd_ = mxq(f64(wd), 0, "e5m2")
    x_ = mxq(f64(x), 0, "e4m3")
    y = w_.T @ xd_ + wd_.T @ x_
    return y

from contextlib import ExitStack

import concourse.mybir as mybir

K, N, T = 512, 2048, 1536
FLOPS = 2 * 2 * K * N * T

F32 = mybir.dt.float32
BF16 = mybir.dt.bfloat16
U32 = mybir.dt.uint32
U8 = mybir.dt.uint8
E4M3 = mybir.dt.float8_e4m3fn_x4
E5M2 = mybir.dt.float8_e5m2_x4

P = 128
PACK = 4
T_TILE = 512
T_TILES = T // T_TILE
ROWS = 2
BLOCK = P * ROWS
BLOCKS = N // BLOCK
WD_CHUNKS = (512, 512, 1024)


def tile_mix_jvp_fm_none_kernel(tc, w, xd, wd, x, out):
    nc = tc.nc
    with ExitStack() as ctx:
        keep = ctx.enter_context(tc.tile_pool(name="keep", bufs=1))
        stage = ctx.enter_context(tc.tile_pool(name="stage", bufs=3))
        results = ctx.enter_context(tc.tile_pool(name="results", bufs=5))
        psum = ctx.enter_context(tc.psum_pool(name="psum", bufs=8))
        ctx.enter_context(tc.manual_schedule())

        def view(a):
            return a.rearrange("(p j) c -> p j c", j=PACK)

        x_raw = keep.tile([P, PACK, T], F32, name="x_raw")
        nc.sync.dma_start(out=x_raw[:], in_=view(x))
        xd_raw = keep.tile([P, PACK, T], F32, name="xd_raw")
        nc.sync.dma_start(out=xd_raw[:], in_=view(xd))
        w_raw = keep.tile([P, PACK, N], F32, name="w_raw")
        nc.sync.dma_start(out=w_raw[:], in_=view(w))
        wd_raw = []
        c0 = 0
        for width in WD_CHUNKS:
            chunk = keep.tile([P, PACK, width], F32, name="wd_raw%d" % c0)
            nc.sync.dma_start(out=chunk[:], in_=view(wd)[:, :, c0 : c0 + width])
            for b in range(width // BLOCK):
                wd_raw.append(chunk[:, :, b * BLOCK : (b + 1) * BLOCK])
            c0 += width

        x_codes = keep.tile([P, T], U32, name="x_codes", align_bytes=64)
        x_scales = keep.tile([P, T], U8, name="x_scales", align_bytes=64)
        xd_codes = keep.tile([P, T], U32, name="xd_codes", align_bytes=64)
        xd_scales = keep.tile([P, T], U8, name="xd_scales", align_bytes=64)

        def copy(engine, dst, src):
            if engine == "v":
                nc.vector.tensor_copy(out=dst, in_=src)
            else:
                nc.scalar.copy(out=dst, in_=src)

        def prepare_moving(raw, codes, scales, fmt):
            staged = {}
            for c, engine in ((0, "v"), (1, "s"), (2, "v")):
                g = stage.tile([P, T_TILE, PACK], BF16, name="g", align_bytes=64)
                copy(
                    engine,
                    g[:].rearrange("p (c i) j -> p c j i", i=4),
                    raw[:, :, c * T_TILE : (c + 1) * T_TILE].rearrange("p j (c i) -> p c j i", i=4),
                )
                staged[c] = g
            for c in (0, 2, 1):
                cols = slice(c * T_TILE, (c + 1) * T_TILE)
                nc.vector.quantize_mx(
                    out=codes[:, cols].bitcast(fmt),
                    scales=scales[:, cols],
                    in_=staged[c][:].rearrange("p c j -> p (c j)"),
                )

        w_staged, wd_staged, w_mx, wd_mx = {}, {}, {}, {}

        def stage_stationary(b, engine, src, staged):
            s = stage.tile([P, ROWS, P, PACK], BF16, name="s", bufs=5, align_bytes=64)
            copy(
                engine,
                s[:].rearrange("p i m j -> p m j i"),
                src.rearrange("p j (m i) -> p m j i", i=ROWS),
            )
            staged[b] = s

        def stage_w(b, engine):
            stage_stationary(b, engine, w_raw[:, :, b * BLOCK : (b + 1) * BLOCK], w_staged)

        def stage_wd(b, engine):
            stage_stationary(b, engine, wd_raw[b], wd_staged)

        def quantise_stationary(b, staged, mx, fmt, label):
            codes = keep.tile([P, BLOCK], U32, name="%s_codes%d" % (label, b), align_bytes=64)
            scales = keep.tile([P, BLOCK], U8, name="%s_scales%d" % (label, b), align_bytes=64)
            nc.vector.quantize_mx(
                out=codes[:].bitcast(fmt),
                scales=scales[:],
                in_=staged[b][:].rearrange("p i m j -> p (i m j)"),
            )
            mx[b] = (codes, scales)

        def quantise_w(b):
            quantise_stationary(b, w_staged, w_mx, E4M3, "w")

        def quantise_wd(b):
            quantise_stationary(b, wd_staged, wd_mx, E5M2, "wd")

        banks = {}

        def multiply(b, i, second):
            codes, scales = wd_mx[b] if second else w_mx[b]
            for c in range(T_TILES):
                if not second:
                    acc = psum.tile([P, T_TILE], F32, name="acc")
                    banks[b, i, c] = acc
                t_cols = slice(c * T_TILE, (c + 1) * T_TILE)
                n_cols = slice(i * P, (i + 1) * P)
                nc.tensor.matmul_mx(
                    out=banks[b, i, c][:],
                    lhsT=codes[:, n_cols].bitcast(E5M2 if second else E4M3),
                    lhsT_scale=scales[:, n_cols],
                    rhs=(x_codes if second else xd_codes)[:, t_cols].bitcast(E4M3 if second else E5M2),
                    rhs_scale=(x_scales if second else xd_scales)[:, t_cols],
                    start=not second,
                    stop=second,
                )

        prepare_moving(x_raw, x_codes, x_scales, E4M3)
        prepare_moving(xd_raw, xd_codes, xd_scales, E5M2)

        stage_w(0, "v")
        stage_w(1, "s")
        stage_w(2, "v")
        quantise_w(0)
        quantise_w(1)
        multiply(0, 0, False)
        multiply(0, 1, False)
        stage_w(3, "s")
        stage_wd(0, "v")
        stage_wd(1, "s")
        quantise_w(2)
        quantise_wd(0)
        multiply(0, 0, True)
        multiply(0, 1, True)
        quantise_wd(1)
        quantise_w(3)

        steps = {
            (0, 1): [lambda: stage_wd(2, "v")],
            (0, 3): [lambda: stage_wd(3, "v"), lambda: quantise_wd(2)],
            (0, 5): [lambda: quantise_wd(3)],
        }
        for b in range(1, 5):
            steps[b, 0] = [lambda b=b: stage_w(b + 3, "v"), lambda b=b: stage_wd(b + 3, "v")]
            steps[b, 2] = [lambda b=b: quantise_w(b + 3)]
            steps[b, 4] = [lambda b=b: quantise_wd(b + 3)]
        vector_banks = {0: (2, 5), 1: (3,), 2: (3,), 3: (3,), 4: (1, 4), 5: (1, 3, 5), 6: (1, 3, 5), 7: (1, 3, 5)}

        out_view = out.rearrange("(b m i) t -> b m i t", m=P, i=ROWS)
        for b in range(BLOCKS):
            result = results.tile([P, ROWS, T], F32, name="result")
            for i in range(ROWS):
                if b > 0:
                    multiply(b, i, False)
                    multiply(b, i, True)
                for c in range(T_TILES):
                    q = i * T_TILES + c
                    copy(
                        "v" if q in vector_banks[b] else "s",
                        result[:, i, c * T_TILE : (c + 1) * T_TILE],
                        banks[b, i, c][:],
                    )
                    for step in steps.get((b, q), []):
                        step()
                if b in (0, BLOCKS - 1):
                    nc.sync.dma_start(out=out_view[b][:, i : i + 1, :], in_=result[:, i : i + 1, :])
            if b not in (0, BLOCKS - 1):
                nc.sync.dma_start(out=out_view[b], in_=result[:])
